import numpy as np
import ml_dtypes


def mxq(x, axis, fmt="e4m3"):
    dtype, down = {"e4m3": (ml_dtypes.float8_e4m3fn, 7), "e5m2": (ml_dtypes.float8_e5m2, 14)}[fmt]
    v = np.moveaxis(np.asarray(x, np.float32).astype(ml_dtypes.bfloat16).astype(np.float64), axis, -1)
    blocks = v.reshape(v.shape[:-1] + (-1, 32))
    amax = np.abs(blocks).max(-1, keepdims=True)
    byte = np.maximum(np.where(amax > 0, np.frexp(amax)[1] - 1 + 127, 0) - down, 1)
    scale = np.exp2(byte - 127.0)
    codes = (blocks / scale).astype(np.float32).astype(dtype).astype(np.float64)
    return np.moveaxis((codes * scale).reshape(v.shape), -1, axis)


WIDE = False


def mx_kscale(k):
    if not WIDE:
        return np.ones(k)
    levels = np.array([10, -10, 5, -5, 0])
    if k % 512:
        return np.exp2(np.random.permutation(np.resize(levels, k // 32))).repeat(32)
    a = np.empty((k // 512, 16))
    for p in range(k // 512):
        a[p, :8] = np.random.permutation(np.resize(levels, 8))
        for g in range(8):
            far = levels[np.abs(levels - a[p, g]) >= 10]
            a[p, g + 8] = far[np.random.randint(len(far))]
    return np.exp2(a.ravel()).repeat(32)


def f64(x):
    return np.asarray(x).astype(np.float64)


def striped(idx):
    return np.tile(idx.reshape(-1, 16).T, (8, 1)).astype(np.uint16)


def unstriped(offs):
    return offs[:16].T.reshape(-1).astype(np.int64)


def striped8(idx):
    return np.concatenate([x.reshape(-1, 16).T for x in idx]).astype(np.uint16)


def runs(offs, k):
    lists = np.stack([offs[16 * r : 16 * r + 16].T.reshape(-1) for r in range(8)]).astype(np.int64)
    return lists[np.arange(k) % 512 // 64]


def pack_weight(w):
    k, n = w.shape
    w = f64(np.asarray(w, np.float32).astype(ml_dtypes.bfloat16)).reshape(k // 32, 32, n)
    amax = np.abs(w).max(1)
    byte = np.clip(np.where(amax > 0, np.frexp(amax)[1] - 1 + 127 - 7, 1), 1, 254)
    scaled = (w * np.exp2(127.0 - byte)[:, None, :]).reshape(k, n).astype(np.float32)
    words = np.ascontiguousarray(scaled.reshape(k // 512, 128, 4, n).transpose(0, 1, 3, 2)).astype(ml_dtypes.float8_e4m3fn).view(np.uint8)
    return words, np.ascontiguousarray(byte.astype(np.uint8).reshape(k // 512, 16, n))


def unpack_weight(words, scales):
    g, p, n, _ = words.shape
    vals = np.ascontiguousarray(words).view(ml_dtypes.float8_e4m3fn).astype(np.float64) * np.repeat(np.exp2(scales.astype(np.float64) - 127.0), 8, axis=1)[..., None]
    return vals.transpose(0, 1, 3, 2).reshape(g * 512, n)


def sigmoid(v):
    return 1.0 / (1.0 + np.exp(-np.maximum(v, -700.0)))

def planes(y):
    n, m = y.shape
    v = y.astype(np.float32).astype(ml_dtypes.bfloat16).astype(np.float64).reshape(n // 32, 32, m)
    top = np.abs(v).max(1)
    byte = np.clip(np.where(top > 0, np.frexp(top)[1] - 1 + 127 - 7, 1), 1, 254)
    codes = (v * np.exp2(127.0 - byte)[:, None, :]).reshape(n, m).astype(np.float32).astype(ml_dtypes.float8_e4m3fn).view(np.uint8)
    words = codes.reshape(n // 512, 128, 4, m).transpose(0, 1, 3, 2)
    return np.ascontiguousarray(words), np.ascontiguousarray(byte.astype(np.uint8).reshape(n // 512, 16, m))


K, T, S, N, H, W, U = 512, 2048, 512, 512, 512, 256, 1024


def setup_inputs():
    n = np.random.standard_normal
    s = mx_kscale(K)[:, None]
    u = mx_kscale(S)
    packed_xT = pack_weight(n((K, T)) * s)
    perm = np.stack([np.random.permutation(H) for _ in range(8)])
    return {
        "x_words": packed_xT[0],
        "x_scales": packed_xT[1],
        "wa": (n((K, H)) / np.sqrt(K) / s).astype(np.float32),
        "wb": (n((K, N)) / np.sqrt(K) / s).astype(np.float32),
        "gt": (np.random.uniform(0.5, 1.5, (S, 1)) * u[:, None]).astype(np.float32),
        "gi": (np.random.uniform(0.5, 1.5, (S, 1)) / u[:, None]).astype(np.float32),
        "mem": n((H, U)).astype(np.float32),
        "offs": striped(np.random.permutation(T)[:S]),
        "two": striped(np.random.permutation(T)[:S]),
        "n1": striped8(perm[:, :W]),
        "n2": striped8(perm[:, W:]),
        "n3": striped8(np.stack([np.random.permutation(U)[:N] for _ in range(8)])),
    }


def reference(x_words, x_scales, wa, wb, gt, gi, mem, offs, two, n1, n2, n3):
    old = f64(mem)[np.arange(H)[:, None], runs(n3, H)]
    xq = unpack_weight(x_words, x_scales)[:, unstriped(offs)]
    a = xq.T @ mxq(f64(wa), 0, "e4m3")
    pa = a[np.arange(S)[:, None], runs(n1, S)]
    pb = a[np.arange(S)[:, None], runs(n2, S)]
    ra = pa * sigmoid(pb)
    ds = a.copy()
    ds[np.arange(S)[:, None], runs(n2, S)] = ra
    z = f64(gt) * ds
    x_two = unpack_weight(x_words, x_scales)[:, unstriped(two)]
    b = x_two.T @ mxq(f64(wb), 0, "e4m3")
    z2 = f64(gi) * b
    cv = 0.0625 * ((mxq(z, 0, "e4m3").T @ mxq(z2, 0, "e4m3")))
    nw = old + sigmoid(cv) * (cv - old)
    out = f64(mem).copy()
    out[np.arange(H)[:, None], runs(n3, H)] = nw
    return (out,) + planes(out)

@@ -1,0 +1,176 @@
+from contextlib import ExitStack
+
+import concourse.mybir as mybir
+
+K, T, S, N, H, W, U = 512, 2048, 512, 512, 512, 256, 1024
+FLOPS = 2 * K * S * H + 2 * K * S * N + 2 * S * H * N
+
+F32 = mybir.dt.float32
+BF16 = mybir.dt.bfloat16
+I32 = mybir.dt.int32
+U32 = mybir.dt.uint32
+U16 = mybir.dt.uint16
+U8 = mybir.dt.uint8
+FP8X4 = mybir.dt.float8_e4m3fn_x4
+ACT = mybir.ActivationFunctionType
+ALU = mybir.AluOpType
+
+P = 128
+PACK = 4
+HALF = 256
+PAGE_ORDER = (2, 0, 1, 3)
+
+
+def tile_picked_momfoldpaget_none_po_kernel(
+    tc, x_words, x_scales, wa, wb, gt, gi, mem, offs, two, n1, n2, n3, out_0, out_1, out_2
+):
+    nc = tc.nc
+    with ExitStack() as ctx:
+        keep = ctx.enter_context(tc.tile_pool(name="keep", bufs=1))
+        psum = ctx.enter_context(tc.psum_pool(name="psum", bufs=1))
+
+        def sbuf(name, shape, dtype):
+            return keep.tile(shape, dtype, name=name, align_bytes=64)
+
+        offs_l = sbuf("offs_l", [P, S // 16], U16)
+        two_l = sbuf("two_l", [P, S // 16], U16)
+        n1_l = sbuf("n1_l", [P, W // 16], U16)
+        n2_l = sbuf("n2_l", [P, W // 16], U16)
+        n3_l = sbuf("n3_l", [P, N // 16], U16)
+        xw = sbuf("xw", [P, T], U32)
+        xs = sbuf("xs", [P, T], U8)
+        wa_raw = [sbuf("wa_raw%d" % h, [P, PACK, HALF], F32) for h in range(2)]
+        wb_raw = sbuf("wb_raw", [P, PACK, N], F32)
+        gt_c = sbuf("gt_c", [P, PACK], F32)
+        gi_c = sbuf("gi_c", [P, PACK], F32)
+        page = [sbuf("page%d" % t, [P, U], F32) for t in range(PACK)]
+
+        nc.vector.memset(xs[:].bitcast(I32), 0)
+        nc.sync.dma_start(offs_l[:], offs)
+        nc.sync.dma_start(two_l[:], two)
+        for q in range(4):
+            nc.scalar.dma_start(xs[32 * q : 32 * q + 4, :].bitcast(I32), x_scales[0, 4 * q : 4 * q + 4, :].bitcast(I32))
+        nc.sync.dma_start(xw[:].bitcast(I32), x_words[0].rearrange("p n t -> p (n t)").bitcast(I32))
+        wa_rows = wa.rearrange("(p j) n -> p j n", j=PACK)
+        for h in range(2):
+            nc.sync.dma_start(wa_raw[h][:], wa_rows[:, :, h * HALF : (h + 1) * HALF])
+        nc.sync.dma_start(n2_l[:], n2)
+        nc.sync.dma_start(n1_l[:], n1)
+        nc.sync.dma_start(wb_raw[:], wb.rearrange("(p j) n -> p j n", j=PACK))
+        nc.sync.dma_start(gi_c[:], gi.rearrange("(p t) o -> p (t o)", t=PACK))
+        nc.sync.dma_start(gt_c[:], gt.rearrange("(p t) o -> p (t o)", t=PACK))
+        nc.sync.dma_start(n3_l[:], n3)
+        mem_rows = mem.rearrange("(p t) u -> p t u", t=PACK)
+        out_rows = out_0.rearrange("(p t) u -> p t u", t=PACK)
+        for t in PAGE_ORDER:
+            nc.sync.dma_start(page[t][:], mem_rows[:, t, :])
+
+        def dealt(tile):
+            return tile[:].rearrange("p (t m) -> p m t", t=PACK)
+
+        xa_w = sbuf("xa_w", [P, S], U32)
+        xa_s = sbuf("xa_s", [P, S], U8)
+        xb_w = sbuf("xb_w", [P, S], U32)
+        xb_s = sbuf("xb_s", [P, S], U8)
+        nc.vector.tensor_copy(dealt(xa_s), xs[:].indirect(offs_l[:]))
+        nc.vector.tensor_copy(dealt(xb_s), xs[:].indirect(two_l[:]))
+        nc.vector.tensor_copy(dealt(xa_w), xw[:].indirect(offs_l[:]))
+
+        def interleave(copy, dst, src):
+            copy(dst.rearrange("p (c i j) -> p c j i", i=4, j=PACK), src.rearrange("p j (c i) -> p c j i", i=4))
+
+        wa_g = [sbuf("wa_g%d" % h, [P, PACK * HALF], BF16) for h in range(2)]
+        wa_w = sbuf("wa_w", [P, H], U32)
+        wa_s = sbuf("wa_s", [P, H], U8)
+        interleave(nc.scalar.copy, wa_g[0][:], wa_raw[0][:])
+        interleave(nc.scalar.copy, wa_g[1][:, : PACK * P], wa_raw[1][:, :, :P])
+        nc.vector.tensor_copy(dealt(xb_w), xw[:].indirect(two_l[:]))
+        interleave(nc.vector.tensor_copy, wa_g[1][:, PACK * P :], wa_raw[1][:, :, P:])
+        for h in range(2):
+            cols = slice(h * HALF, (h + 1) * HALF)
+            nc.vector.quantize_mx(wa_w[:, cols].bitcast(FP8X4), wa_s[:, cols], wa_g[h][:])
+
+        def product(acc, lw, ls, t, rw, rs):
+            cols = slice(t * P, (t + 1) * P)
+            nc.tensor.matmul_mx(acc, lhsT=lw[:, cols].bitcast(FP8X4), lhsT_scale=ls[:, cols],
+                                rhs=rw.bitcast(FP8X4), rhs_scale=rs, start=True, stop=True)
+
+        a_ps = [psum.tile([P, H], F32, name="a_ps%d" % t, tag="bank%d" % t) for t in range(PACK)]
+        for t in range(PACK):
+            product(a_ps[t][:], xa_w, xa_s, t, wa_w[:], wa_s[:])
+
+        wb_g = sbuf("wb_g", [P, PACK * N], BF16)
+        wb_w = sbuf("wb_w", [P, N], U32)
+        wb_s = sbuf("wb_s", [P, N], U8)
+        interleave(nc.vector.tensor_copy, wb_g[:], wb_raw[:])
+        nc.vector.quantize_mx(wb_w[:].bitcast(FP8X4), wb_s[:], wb_g[:])
+        b_ps = [psum.tile([P, PACK, P], F32, name="b_ps%d" % c, tag="bank%d" % (PACK + c)) for c in range(N // P)]
+        for c in range(N // P):
+            cols = slice(c * P, (c + 1) * P)
+            for t in range(PACK):
+                product(b_ps[c][:, t, :], xb_w, xb_s, t, wb_w[:, cols], wb_s[:, cols])
+
+        ds = [sbuf("ds%d" % t, [P, H], F32) for t in range(PACK)]
+        pa = [sbuf("pa%d" % t, [P, W], F32) for t in range(PACK)]
+        sg = [sbuf("sg%d" % t, [P, W], F32) for t in range(PACK)]
+        z_rows = sbuf("z_rows", [P, PACK, H], BF16)
+        for t in range(PACK):
+            nc.scalar.copy(ds[t][:], a_ps[t][:])
+            nc.scalar.activation(sg[t][:], ds[t][:].indirect(n2_l[:]), ACT.Sigmoid)
+            nc.scalar.activation(pa[t][:], ds[t][:].indirect(n1_l[:]), ACT.Copy)
+            nc.vector.tensor_tensor(ds[t][:].indirect(n2_l[:]), pa[t][:], sg[t][:], ALU.mult)
+        for t in range(PACK):
+            nc.scalar.activation(z_rows[:, t, :], ds[t][:], ACT.Copy, scale=gt_c[:, t : t + 1])
+
+        z2_g = sbuf("z2_g", [P, PACK * N], BF16)
+        z2_w = sbuf("z2_w", [P, N], U32)
+        z2_s = sbuf("z2_s", [P, N], U8)
+        gi_wide = gi_c[:].unsqueeze(1).to_broadcast([P, P, PACK])
+        for c in range(N // P):
+            chunk = z2_g[:, c * PACK * P : (c + 1) * PACK * P].rearrange("p (n t) -> p n t", t=PACK)
+            nc.vector.tensor_tensor(chunk, b_ps[c][:].rearrange("p t n -> p n t"), gi_wide, ALU.mult)
+        nc.vector.quantize_mx(z2_w[:].bitcast(FP8X4), z2_s[:], z2_g[:])
+
+        old_h = [sbuf("old_h%d" % t, [P, N], F32) for t in range(PACK)]
+        nc.scalar.activation(old_h[PAGE_ORDER[0]][:], page[PAGE_ORDER[0]][:].indirect(n3_l[:]), ACT.Copy, scale=-0.5)
+
+        z_g = [sbuf("z_g%d" % t, [P, PACK * P], BF16) for t in range(PACK)]
+        z_w = [sbuf("z_w%d" % t, [P, P], U32) for t in range(PACK)]
+        z_s = [sbuf("z_s%d" % t, [P, P], U8) for t in range(PACK)]
+        c_ps = [psum.tile([P, N], F32, name="c_ps%d" % t, tag="bank%d" % t) for t in range(PACK)]
+        z_dealt = z_rows[:].rearrange("p j (m t) -> p t m j", t=PACK)
+        for t in PAGE_ORDER:
+            nc.vector.tensor_copy(z_g[t][:].rearrange("p (m j) -> p m j", j=PACK), z_dealt[:, t, :, :])
+        for t in PAGE_ORDER:
+            nc.vector.quantize_mx(z_w[t][:].bitcast(FP8X4), z_s[t][:], z_g[t][:])
+            product(c_ps[t][:], z_w[t], z_s[t], 0, z2_w[:], z2_s[:])
+
+        th = [sbuf("th%d" % t, [P, N], F32) for t in range(PACK)]
+        su = [sbuf("su%d" % t, [P, N], F32) for t in range(PACK)]
+        kept = [sbuf("kept%d" % t, [P, N], F32) for t in range(PACK)]
+        y_g = sbuf("y_g", [P, U, PACK], BF16)
+        for i, t in enumerate(PAGE_ORDER):
+            if i == PACK - 1:
+                nc.scalar.copy(y_g[:, :, PAGE_ORDER[0]], page[PAGE_ORDER[0]][:])
+            nc.scalar.activation(th[t][:], c_ps[t][:], ACT.Tanh, scale=0.03125)
+            nc.scalar.activation(su[t][:], c_ps[t][:], ACT.Silu, scale=0.0625)
+            if i > 0:
+                nc.scalar.activation(old_h[t][:], page[t][:].indirect(n3_l[:]), ACT.Copy, scale=-0.5)
+            nc.vector.scalar_tensor_tensor(kept[t][:], th[t][:], -1.0, old_h[t][:], ALU.add, ALU.mult)
+            nc.vector.tensor_tensor(page[t][:].indirect(n3_l[:]), su[t][:], kept[t][:], ALU.add)
+            nc.sync.dma_start(out_rows[:, t, :], page[t][:])
+        nc.scalar.copy(y_g[:, :, PAGE_ORDER[1]], page[PAGE_ORDER[1]][:])
+
+        y_w = sbuf("y_w", [P, U], U32)
+        y_s = sbuf("y_s", [P, U], U8)
+        y_flat = y_g[:].rearrange("p c j -> p (c j)")
+        words_out = out_1[0].rearrange("p c r -> p (c r)").bitcast(I32)
+        for h in range(2):
+            cols = slice(h * 512, (h + 1) * 512)
+            nc.scalar.copy(y_g[:, cols, PAGE_ORDER[2]], page[PAGE_ORDER[2]][:, cols])
+            nc.vector.tensor_copy(y_g[:, cols, PAGE_ORDER[3]], page[PAGE_ORDER[3]][:, cols])
+            nc.vector.quantize_mx(y_w[:, cols].bitcast(FP8X4), y_s[:, cols], y_flat[:, h * 2048 : (h + 1) * 2048])
+            nc.sync.dma_start(words_out[:, cols], y_w[:, cols].bitcast(I32))
+        for q in range(4):
+            queue = nc.scalar if q % 2 else nc.sync
+            queue.dma_start(out_2[0, 4 * q : 4 * q + 4, :].bitcast(I32), y_s[32 * q : 32 * q + 4, :].bitcast(I32))

@@ -17,8 +17,12 @@ ALU = mybir.AluOpType
 
 P = 128
 PACK = 4
+QUADS = 4
+PER_COL = 16
 HALF = 256
-PAGE_ORDER = (2, 0, 1, 3)
+CV_SCALE = 0.0625
+PAGE_ORDER = (3, 0, 1, 2)
+Y_CHUNKS = ((0, 512), (512, 768), (768, 1024))
 
 
 def tile_picked_momfoldpaget_none_po_kernel(
@@ -29,34 +33,62 @@ def tile_picked_momfoldpaget_none_po_kernel(
         keep = ctx.enter_context(tc.tile_pool(name="keep", bufs=1))
         psum = ctx.enter_context(tc.psum_pool(name="psum", bufs=1))
 
-        def sbuf(name, shape, dtype):
-            return keep.tile(shape, dtype, name=name, align_bytes=64)
+        def sbuf(name, shape, dtype, reuse=None):
+            return keep.tile(shape, dtype, name=name, tag=reuse or name, align_bytes=64)
 
-        offs_l = sbuf("offs_l", [P, S // 16], U16)
-        two_l = sbuf("two_l", [P, S // 16], U16)
-        n1_l = sbuf("n1_l", [P, W // 16], U16)
-        n2_l = sbuf("n2_l", [P, W // 16], U16)
-        n3_l = sbuf("n3_l", [P, N // 16], U16)
+        def scalar_copy(out, in_):
+            nc.scalar.activation(out, in_, ACT.Copy)
+
+        def dealt(tile):
+            return tile[:].rearrange("p (t m) -> p m t", t=PACK)
+
+        def interleave(copy, dst, src):
+            copy(dst.rearrange("p (c i j) -> p c j i", i=4, j=PACK), src.rearrange("p j (c i) -> p c j i", i=4))
+
+        def product(acc, lhs_words, lhs_scales, block, rhs_words, rhs_scales):
+            cols = slice(block * P, (block + 1) * P)
+            nc.tensor.matmul_mx(
+                acc,
+                lhsT=lhs_words[:, cols].bitcast(FP8X4),
+                lhsT_scale=lhs_scales[:, cols],
+                rhs=rhs_words.bitcast(FP8X4),
+                rhs_scale=rhs_scales,
+                start=True,
+                stop=True,
+            )
+
+        offs_l = sbuf("offs_l", [P, S // PER_COL], U16)
+        two_l = sbuf("two_l", [P, S // PER_COL], U16)
+        n1_l = sbuf("n1_l", [P, W // PER_COL], U16)
+        n2_l = sbuf("n2_l", [P, W // PER_COL], U16)
+        n3_l = sbuf("n3_l", [P, N // PER_COL], U16)
         xw = sbuf("xw", [P, T], U32)
         xs = sbuf("xs", [P, T], U8)
         wa_raw = [sbuf("wa_raw%d" % h, [P, PACK, HALF], F32) for h in range(2)]
-        wb_raw = sbuf("wb_raw", [P, PACK, N], F32)
+        wb_raw = [sbuf("wb_raw%d" % h, [P, PACK, HALF], F32) for h in range(2)]
         gt_c = sbuf("gt_c", [P, PACK], F32)
         gi_c = sbuf("gi_c", [P, PACK], F32)
         page = [sbuf("page%d" % t, [P, U], F32) for t in range(PACK)]
 
+        warm_in = sbuf("warm_in", [P, 1], F32)
+        warm_sigmoid = sbuf("warm_sigmoid", [P, 1], F32)
+        nc.gpsimd.memset(warm_in[:], 0.0)
+        nc.scalar.activation(warm_sigmoid[:], warm_in[:], ACT.Sigmoid)
+
         nc.vector.memset(xs[:].bitcast(I32), 0)
         nc.sync.dma_start(offs_l[:], offs)
         nc.sync.dma_start(two_l[:], two)
-        for q in range(4):
-            nc.scalar.dma_start(xs[32 * q : 32 * q + 4, :].bitcast(I32), x_scales[0, 4 * q : 4 * q + 4, :].bitcast(I32))
+        nc.sync.dma_start(n2_l[:], n2)
+        for q in range(QUADS):
+            nc.sync.dma_start(xs[32 * q : 32 * q + 4, :].bitcast(I32), x_scales[0, 4 * q : 4 * q + 4, :].bitcast(I32))
         nc.sync.dma_start(xw[:].bitcast(I32), x_words[0].rearrange("p n t -> p (n t)").bitcast(I32))
         wa_rows = wa.rearrange("(p j) n -> p j n", j=PACK)
         for h in range(2):
             nc.sync.dma_start(wa_raw[h][:], wa_rows[:, :, h * HALF : (h + 1) * HALF])
-        nc.sync.dma_start(n2_l[:], n2)
+        wb_rows = wb.rearrange("(p j) n -> p j n", j=PACK)
+        for h in range(2):
+            nc.sync.dma_start(wb_raw[h][:], wb_rows[:, :, h * HALF : (h + 1) * HALF])
         nc.sync.dma_start(n1_l[:], n1)
-        nc.sync.dma_start(wb_raw[:], wb.rearrange("(p j) n -> p j n", j=PACK))
         nc.sync.dma_start(gi_c[:], gi.rearrange("(p t) o -> p (t o)", t=PACK))
         nc.sync.dma_start(gt_c[:], gt.rearrange("(p t) o -> p (t o)", t=PACK))
         nc.sync.dma_start(n3_l[:], n3)
@@ -64,9 +96,6 @@ def tile_picked_momfoldpaget_none_po_kernel(
         out_rows = out_0.rearrange("(p t) u -> p t u", t=PACK)
         for t in PAGE_ORDER:
             nc.sync.dma_start(page[t][:], mem_rows[:, t, :])
-
-        def dealt(tile):
-            return tile[:].rearrange("p (t m) -> p m t", t=PACK)
 
         xa_w = sbuf("xa_w", [P, S], U32)
         xa_s = sbuf("xa_s", [P, S], U8)
@@ -76,53 +105,50 @@ def tile_picked_momfoldpaget_none_po_kernel(
         nc.vector.tensor_copy(dealt(xb_s), xs[:].indirect(two_l[:]))
         nc.vector.tensor_copy(dealt(xa_w), xw[:].indirect(offs_l[:]))
 
-        def interleave(copy, dst, src):
-            copy(dst.rearrange("p (c i j) -> p c j i", i=4, j=PACK), src.rearrange("p j (c i) -> p c j i", i=4))
-
         wa_g = [sbuf("wa_g%d" % h, [P, PACK * HALF], BF16) for h in range(2)]
         wa_w = sbuf("wa_w", [P, H], U32)
         wa_s = sbuf("wa_s", [P, H], U8)
-        interleave(nc.scalar.copy, wa_g[0][:], wa_raw[0][:])
-        interleave(nc.scalar.copy, wa_g[1][:, : PACK * P], wa_raw[1][:, :, :P])
+        interleave(scalar_copy, wa_g[0][:], wa_raw[0][:])
+        interleave(scalar_copy, wa_g[1][:, : PACK * P], wa_raw[1][:, :, :P])
         nc.vector.tensor_copy(dealt(xb_w), xw[:].indirect(two_l[:]))
         interleave(nc.vector.tensor_copy, wa_g[1][:, PACK * P :], wa_raw[1][:, :, P:])
         for h in range(2):
             cols = slice(h * HALF, (h + 1) * HALF)
             nc.vector.quantize_mx(wa_w[:, cols].bitcast(FP8X4), wa_s[:, cols], wa_g[h][:])
 
-        def product(acc, lw, ls, t, rw, rs):
-            cols = slice(t * P, (t + 1) * P)
-            nc.tensor.matmul_mx(acc, lhsT=lw[:, cols].bitcast(FP8X4), lhsT_scale=ls[:, cols],
-                                rhs=rw.bitcast(FP8X4), rhs_scale=rs, start=True, stop=True)
-
-        a_ps = [psum.tile([P, H], F32, name="a_ps%d" % t, tag="bank%d" % t) for t in range(PACK)]
+        ds = [sbuf("ds%d" % t, [P, H], F32) for t in range(PACK)]
+        wb_g0 = sbuf("wb_g0", [P, PACK * HALF], BF16)
+        interleave(scalar_copy, wb_g0[:], wb_raw[0][:])
+        a_ps = [psum.tile([P, H], F32, name="a_ps%d" % t, tag="bank%d" % (PACK + t)) for t in range(PACK)]
         for t in range(PACK):
             product(a_ps[t][:], xa_w, xa_s, t, wa_w[:], wa_s[:])
-
-        wb_g = sbuf("wb_g", [P, PACK * N], BF16)
         wb_w = sbuf("wb_w", [P, N], U32)
         wb_s = sbuf("wb_s", [P, N], U8)
-        interleave(nc.vector.tensor_copy, wb_g[:], wb_raw[:])
-        nc.vector.quantize_mx(wb_w[:].bitcast(FP8X4), wb_s[:], wb_g[:])
-        b_ps = [psum.tile([P, PACK, P], F32, name="b_ps%d" % c, tag="bank%d" % (PACK + c)) for c in range(N // P)]
+        wb_g1 = sbuf("wb_g1", [P, PACK * HALF], BF16, reuse="wa_g1")
+        interleave(nc.vector.tensor_copy, wb_g1[:], wb_raw[1][:])
+        for h, grouped in enumerate((wb_g0, wb_g1)):
+            cols = slice(h * HALF, (h + 1) * HALF)
+            nc.vector.quantize_mx(wb_w[:, cols].bitcast(FP8X4), wb_s[:, cols], grouped[:])
+
+        b_ps = [psum.tile([P, PACK, P], F32, name="b_ps%d" % c, tag="bank%d" % c) for c in range(N // P)]
         for c in range(N // P):
             cols = slice(c * P, (c + 1) * P)
             for t in range(PACK):
                 product(b_ps[c][:, t, :], xb_w, xb_s, t, wb_w[:, cols], wb_s[:, cols])
 
-        ds = [sbuf("ds%d" % t, [P, H], F32) for t in range(PACK)]
         pa = [sbuf("pa%d" % t, [P, W], F32) for t in range(PACK)]
         sg = [sbuf("sg%d" % t, [P, W], F32) for t in range(PACK)]
         z_rows = sbuf("z_rows", [P, PACK, H], BF16)
         for t in range(PACK):
             nc.scalar.copy(ds[t][:], a_ps[t][:])
             nc.scalar.activation(sg[t][:], ds[t][:].indirect(n2_l[:]), ACT.Sigmoid)
-            nc.scalar.activation(pa[t][:], ds[t][:].indirect(n1_l[:]), ACT.Copy)
+            fetch = nc.vector.tensor_copy if t == 0 else scalar_copy
+            fetch(pa[t][:], ds[t][:].indirect(n1_l[:]))
             nc.vector.tensor_tensor(ds[t][:].indirect(n2_l[:]), pa[t][:], sg[t][:], ALU.mult)
         for t in range(PACK):
             nc.scalar.activation(z_rows[:, t, :], ds[t][:], ACT.Copy, scale=gt_c[:, t : t + 1])
 
-        z2_g = sbuf("z2_g", [P, PACK * N], BF16)
+        z2_g = sbuf("z2_g", [P, PACK * N], BF16, reuse="sg%d" % (PACK - 1))
         z2_w = sbuf("z2_w", [P, N], U32)
         z2_s = sbuf("z2_s", [P, N], U8)
         gi_wide = gi_c[:].unsqueeze(1).to_broadcast([P, P, PACK])
@@ -131,46 +157,77 @@ def tile_picked_momfoldpaget_none_po_kernel(
             nc.vector.tensor_tensor(chunk, b_ps[c][:].rearrange("p t n -> p n t"), gi_wide, ALU.mult)
         nc.vector.quantize_mx(z2_w[:].bitcast(FP8X4), z2_s[:], z2_g[:])
 
-        old_h = [sbuf("old_h%d" % t, [P, N], F32) for t in range(PACK)]
-        nc.scalar.activation(old_h[PAGE_ORDER[0]][:], page[PAGE_ORDER[0]][:].indirect(n3_l[:]), ACT.Copy, scale=-0.5)
+        z_dealt = z_rows[:].rearrange("p j (m t) -> p m t j", t=PACK)
+        c_ps = {}
+        col_parts = {t: ((0, N),) for t in PAGE_ORDER}
+        col_parts[PAGE_ORDER[0]] = ((0, HALF), (HALF, N))
+        for name, copy, tiles in (("first", nc.scalar.copy, PAGE_ORDER[:1]), ("rest", nc.vector.tensor_copy, PAGE_ORDER[1:])):
+            n_t = len(tiles)
+            z_g = sbuf("z_g_" + name, [P, n_t * PACK * P], BF16)
+            z_w = sbuf("z_w_" + name, [P, n_t * P], U32)
+            z_s = sbuf("z_s_" + name, [P, n_t * P], U8)
+            copy(z_g[:].rearrange("p (t m j) -> p m t j", t=n_t, j=PACK), z_dealt[:, :, tiles[0] : tiles[0] + n_t, :])
+            nc.vector.quantize_mx(z_w[:].bitcast(FP8X4), z_s[:], z_g[:])
+            for i, t in enumerate(tiles):
+                for c0, c1 in col_parts[t]:
+                    c_ps[t, c0] = psum.tile([P, c1 - c0], F32, name="c_ps%d_%d" % (t, c0), tag="bank%d" % (t + c0 // HALF))
+                    product(c_ps[t, c0][:], z_w, z_s, i, z2_w[:, c0:c1], z2_s[:, c0:c1])
 
-        z_g = [sbuf("z_g%d" % t, [P, PACK * P], BF16) for t in range(PACK)]
-        z_w = [sbuf("z_w%d" % t, [P, P], U32) for t in range(PACK)]
-        z_s = [sbuf("z_s%d" % t, [P, P], U8) for t in range(PACK)]
-        c_ps = [psum.tile([P, N], F32, name="c_ps%d" % t, tag="bank%d" % t) for t in range(PACK)]
-        z_dealt = z_rows[:].rearrange("p j (m t) -> p t m j", t=PACK)
-        for t in PAGE_ORDER:
-            nc.vector.tensor_copy(z_g[t][:].rearrange("p (m j) -> p m j", j=PACK), z_dealt[:, t, :, :])
-        for t in PAGE_ORDER:
-            nc.vector.quantize_mx(z_w[t][:].bitcast(FP8X4), z_s[t][:], z_g[t][:])
-            product(c_ps[t][:], z_w[t], z_s[t], 0, z2_w[:], z2_s[:])
+        warm_silu = sbuf("warm_silu", [P, 1], F32)
+        nc.scalar.activation(warm_silu[:], z_rows[:, PACK - 1, 0:1], ACT.Silu)
 
+        old_buffers = dict(zip(PAGE_ORDER, ("pa%d" % (PACK - 2), "z_g_rest", "z_w_rest", "z_s_rest")))
+        old_h = {}
+
+        def fetch_old(t):
+            old_h[t] = sbuf("old_h%d" % t, [P, N], F32, reuse=old_buffers[t])
+            nc.scalar.activation(old_h[t][:], page[t][:].indirect(n3_l[:]), ACT.Copy, scale=-0.5)
+
+        fetch_old(PAGE_ORDER[0])
         th = [sbuf("th%d" % t, [P, N], F32) for t in range(PACK)]
         su = [sbuf("su%d" % t, [P, N], F32) for t in range(PACK)]
         kept = [sbuf("kept%d" % t, [P, N], F32) for t in range(PACK)]
         y_g = sbuf("y_g", [P, U, PACK], BF16)
-        for i, t in enumerate(PAGE_ORDER):
-            if i == PACK - 1:
-                nc.scalar.copy(y_g[:, :, PAGE_ORDER[0]], page[PAGE_ORDER[0]][:])
-            nc.scalar.activation(th[t][:], c_ps[t][:], ACT.Tanh, scale=0.03125)
-            nc.scalar.activation(su[t][:], c_ps[t][:], ACT.Silu, scale=0.0625)
-            if i > 0:
-                nc.scalar.activation(old_h[t][:], page[t][:].indirect(n3_l[:]), ACT.Copy, scale=-0.5)
-            nc.vector.scalar_tensor_tensor(kept[t][:], th[t][:], -1.0, old_h[t][:], ALU.add, ALU.mult)
-            nc.vector.tensor_tensor(page[t][:].indirect(n3_l[:]), su[t][:], kept[t][:], ALU.add)
+
+        def keep_part(t):
+            for c0, c1 in col_parts[t]:
+                nc.scalar.activation(th[t][:, c0:c1], c_ps[t, c0][:], ACT.Tanh, scale=CV_SCALE / 2)
+            if t not in old_h:
+                fetch_old(t)
+            for c0, c1 in col_parts[t]:
+                nc.vector.scalar_tensor_tensor(kept[t][:, c0:c1], th[t][:, c0:c1], -1.0, old_h[t][:, c0:c1], ALU.add, ALU.mult)
+
+        def write_part(t):
+            for c0, c1 in col_parts[t]:
+                nc.scalar.activation(su[t][:, c0:c1], c_ps[t, c0][:], ACT.Silu, scale=CV_SCALE)
+                slots = page[t][:].indirect(n3_l[:, c0 // PER_COL : c1 // PER_COL])
+                nc.vector.tensor_tensor(slots, su[t][:, c0:c1], kept[t][:, c0:c1], ALU.add)
             nc.sync.dma_start(out_rows[:, t, :], page[t][:])
-        nc.scalar.copy(y_g[:, :, PAGE_ORDER[1]], page[PAGE_ORDER[1]][:])
+
+        def round_slot(copy, t, cols):
+            copy(y_g[:, cols, t], page[t][:, cols])
+
+        first, second, third, last = PAGE_ORDER
+        keep_part(first)
+        write_part(first)
+        keep_part(second)
+        for t, t_next in ((second, third), (third, last)):
+            keep_part(t_next)
+            write_part(t)
+        round_slot(nc.scalar.copy, first, slice(0, U))
+        write_part(last)
+        round_slot(nc.scalar.copy, second, slice(0, U))
 
         y_w = sbuf("y_w", [P, U], U32)
         y_s = sbuf("y_s", [P, U], U8)
         y_flat = y_g[:].rearrange("p c j -> p (c j)")
         words_out = out_1[0].rearrange("p c r -> p (c r)").bitcast(I32)
-        for h in range(2):
-            cols = slice(h * 512, (h + 1) * 512)
-            nc.scalar.copy(y_g[:, cols, PAGE_ORDER[2]], page[PAGE_ORDER[2]][:, cols])
-            nc.vector.tensor_copy(y_g[:, cols, PAGE_ORDER[3]], page[PAGE_ORDER[3]][:, cols])
-            nc.vector.quantize_mx(y_w[:, cols].bitcast(FP8X4), y_s[:, cols], y_flat[:, h * 2048 : (h + 1) * 2048])
+        for c0, c1 in Y_CHUNKS:
+            cols = slice(c0, c1)
+            round_slot(nc.scalar.copy, third, cols)
+            round_slot(nc.scalar.copy if c1 == U else nc.vector.tensor_copy, last, cols)
+            nc.vector.quantize_mx(y_w[:, cols].bitcast(FP8X4), y_s[:, cols], y_flat[:, PACK * c0 : PACK * c1])
             nc.sync.dma_start(words_out[:, cols], y_w[:, cols].bitcast(I32))
-        for q in range(4):
+        for q in range(QUADS):
             queue = nc.scalar if q % 2 else nc.sync
             queue.dma_start(out_2[0, 4 * q : 4 * q + 4, :].bitcast(I32), y_s[32 * q : 32 * q + 4, :].bitcast(I32))

from contextlib import ExitStack

import concourse.mybir as mybir

K, T, S, N, H, W, U = 512, 2048, 512, 512, 512, 256, 1024
FLOPS = 2 * K * S * H + 2 * K * S * N + 2 * S * H * N

F32 = mybir.dt.float32
BF16 = mybir.dt.bfloat16
I32 = mybir.dt.int32
U32 = mybir.dt.uint32
U16 = mybir.dt.uint16
U8 = mybir.dt.uint8
FP8X4 = mybir.dt.float8_e4m3fn_x4
ACT = mybir.ActivationFunctionType
ALU = mybir.AluOpType

P = 128
PACK = 4
QUADS = 4
PER_COL = 16
HALF = 256
CV_SCALE = 0.0625
PAGE_ORDER = (3, 0, 1, 2)
Y_CHUNKS = ((0, 512), (512, 768), (768, 1024))


def tile_picked_momfoldpaget_none_po_kernel(
    tc, x_words, x_scales, wa, wb, gt, gi, mem, offs, two, n1, n2, n3, out_0, out_1, out_2
):
    nc = tc.nc
    with ExitStack() as ctx:
        keep = ctx.enter_context(tc.tile_pool(name="keep", bufs=1))
        psum = ctx.enter_context(tc.psum_pool(name="psum", bufs=1))

        def sbuf(name, shape, dtype, reuse=None):
            return keep.tile(shape, dtype, name=name, tag=reuse or name, align_bytes=64)

        def scalar_copy(out, in_):
            nc.scalar.activation(out, in_, ACT.Copy)

        def dealt(tile):
            return tile[:].rearrange("p (t m) -> p m t", t=PACK)

        def interleave(copy, dst, src):
            copy(dst.rearrange("p (c i j) -> p c j i", i=4, j=PACK), src.rearrange("p j (c i) -> p c j i", i=4))

        def product(acc, lhs_words, lhs_scales, block, rhs_words, rhs_scales):
            cols = slice(block * P, (block + 1) * P)
            nc.tensor.matmul_mx(
                acc,
                lhsT=lhs_words[:, cols].bitcast(FP8X4),
                lhsT_scale=lhs_scales[:, cols],
                rhs=rhs_words.bitcast(FP8X4),
                rhs_scale=rhs_scales,
                start=True,
                stop=True,
            )

        offs_l = sbuf("offs_l", [P, S // PER_COL], U16)
        two_l = sbuf("two_l", [P, S // PER_COL], U16)
        n1_l = sbuf("n1_l", [P, W // PER_COL], U16)
        n2_l = sbuf("n2_l", [P, W // PER_COL], U16)
        n3_l = sbuf("n3_l", [P, N // PER_COL], U16)
        xw = sbuf("xw", [P, T], U32)
        xs = sbuf("xs", [P, T], U8)
        wa_raw = [sbuf("wa_raw%d" % h, [P, PACK, HALF], F32) for h in range(2)]
        wb_raw = [sbuf("wb_raw%d" % h, [P, PACK, HALF], F32) for h in range(2)]
        gt_c = sbuf("gt_c", [P, PACK], F32)
        gi_c = sbuf("gi_c", [P, PACK], F32)
        page = [sbuf("page%d" % t, [P, U], F32) for t in range(PACK)]

        warm_in = sbuf("warm_in", [P, 1], F32)
        warm_sigmoid = sbuf("warm_sigmoid", [P, 1], F32)
        nc.gpsimd.memset(warm_in[:], 0.0)
        nc.scalar.activation(warm_sigmoid[:], warm_in[:], ACT.Sigmoid)

        nc.vector.memset(xs[:].bitcast(I32), 0)
        nc.sync.dma_start(offs_l[:], offs)
        nc.sync.dma_start(two_l[:], two)
        nc.sync.dma_start(n2_l[:], n2)
        for q in range(QUADS):
            nc.sync.dma_start(xs[32 * q : 32 * q + 4, :].bitcast(I32), x_scales[0, 4 * q : 4 * q + 4, :].bitcast(I32))
        nc.sync.dma_start(xw[:].bitcast(I32), x_words[0].rearrange("p n t -> p (n t)").bitcast(I32))
        wa_rows = wa.rearrange("(p j) n -> p j n", j=PACK)
        for h in range(2):
            nc.sync.dma_start(wa_raw[h][:], wa_rows[:, :, h * HALF : (h + 1) * HALF])
        wb_rows = wb.rearrange("(p j) n -> p j n", j=PACK)
        for h in range(2):
            nc.sync.dma_start(wb_raw[h][:], wb_rows[:, :, h * HALF : (h + 1) * HALF])
        nc.sync.dma_start(n1_l[:], n1)
        nc.sync.dma_start(gi_c[:], gi.rearrange("(p t) o -> p (t o)", t=PACK))
        nc.sync.dma_start(gt_c[:], gt.rearrange("(p t) o -> p (t o)", t=PACK))
        nc.sync.dma_start(n3_l[:], n3)
        mem_rows = mem.rearrange("(p t) u -> p t u", t=PACK)
        out_rows = out_0.rearrange("(p t) u -> p t u", t=PACK)
        for t in PAGE_ORDER:
            nc.sync.dma_start(page[t][:], mem_rows[:, t, :])

        xa_w = sbuf("xa_w", [P, S], U32)
        xa_s = sbuf("xa_s", [P, S], U8)
        xb_w = sbuf("xb_w", [P, S], U32)
        xb_s = sbuf("xb_s", [P, S], U8)
        nc.vector.tensor_copy(dealt(xa_s), xs[:].indirect(offs_l[:]))
        nc.vector.tensor_copy(dealt(xb_s), xs[:].indirect(two_l[:]))
        nc.vector.tensor_copy(dealt(xa_w), xw[:].indirect(offs_l[:]))

        wa_g = [sbuf("wa_g%d" % h, [P, PACK * HALF], BF16) for h in range(2)]
        wa_w = sbuf("wa_w", [P, H], U32)
        wa_s = sbuf("wa_s", [P, H], U8)
        interleave(scalar_copy, wa_g[0][:], wa_raw[0][:])
        interleave(scalar_copy, wa_g[1][:, : PACK * P], wa_raw[1][:, :, :P])
        nc.vector.tensor_copy(dealt(xb_w), xw[:].indirect(two_l[:]))
        interleave(nc.vector.tensor_copy, wa_g[1][:, PACK * P :], wa_raw[1][:, :, P:])
        for h in range(2):
            cols = slice(h * HALF, (h + 1) * HALF)
            nc.vector.quantize_mx(wa_w[:, cols].bitcast(FP8X4), wa_s[:, cols], wa_g[h][:])

        ds = [sbuf("ds%d" % t, [P, H], F32) for t in range(PACK)]
        wb_g0 = sbuf("wb_g0", [P, PACK * HALF], BF16)
        interleave(scalar_copy, wb_g0[:], wb_raw[0][:])
        a_ps = [psum.tile([P, H], F32, name="a_ps%d" % t, tag="bank%d" % (PACK + t)) for t in range(PACK)]
        for t in range(PACK):
            product(a_ps[t][:], xa_w, xa_s, t, wa_w[:], wa_s[:])
        wb_w = sbuf("wb_w", [P, N], U32)
        wb_s = sbuf("wb_s", [P, N], U8)
        wb_g1 = sbuf("wb_g1", [P, PACK * HALF], BF16, reuse="wa_g1")
        interleave(nc.vector.tensor_copy, wb_g1[:], wb_raw[1][:])
        for h, grouped in enumerate((wb_g0, wb_g1)):
            cols = slice(h * HALF, (h + 1) * HALF)
            nc.vector.quantize_mx(wb_w[:, cols].bitcast(FP8X4), wb_s[:, cols], grouped[:])

        b_ps = [psum.tile([P, PACK, P], F32, name="b_ps%d" % c, tag="bank%d" % c) for c in range(N // P)]
        for c in range(N // P):
            cols = slice(c * P, (c + 1) * P)
            for t in range(PACK):
                product(b_ps[c][:, t, :], xb_w, xb_s, t, wb_w[:, cols], wb_s[:, cols])

        pa = [sbuf("pa%d" % t, [P, W], F32) for t in range(PACK)]
        sg = [sbuf("sg%d" % t, [P, W], F32) for t in range(PACK)]
        z_rows = sbuf("z_rows", [P, PACK, H], BF16)
        for t in range(PACK):
            nc.scalar.copy(ds[t][:], a_ps[t][:])
            nc.scalar.activation(sg[t][:], ds[t][:].indirect(n2_l[:]), ACT.Sigmoid)
            fetch = nc.vector.tensor_copy if t == 0 else scalar_copy
            fetch(pa[t][:], ds[t][:].indirect(n1_l[:]))
            nc.vector.tensor_tensor(ds[t][:].indirect(n2_l[:]), pa[t][:], sg[t][:], ALU.mult)
        for t in range(PACK):
            nc.scalar.activation(z_rows[:, t, :], ds[t][:], ACT.Copy, scale=gt_c[:, t : t + 1])

        z2_g = sbuf("z2_g", [P, PACK * N], BF16, reuse="sg%d" % (PACK - 1))
        z2_w = sbuf("z2_w", [P, N], U32)
        z2_s = sbuf("z2_s", [P, N], U8)
        gi_wide = gi_c[:].unsqueeze(1).to_broadcast([P, P, PACK])
        for c in range(N // P):
            chunk = z2_g[:, c * PACK * P : (c + 1) * PACK * P].rearrange("p (n t) -> p n t", t=PACK)
            nc.vector.tensor_tensor(chunk, b_ps[c][:].rearrange("p t n -> p n t"), gi_wide, ALU.mult)
        nc.vector.quantize_mx(z2_w[:].bitcast(FP8X4), z2_s[:], z2_g[:])

        z_dealt = z_rows[:].rearrange("p j (m t) -> p m t j", t=PACK)
        c_ps = {}
        col_parts = {t: ((0, N),) for t in PAGE_ORDER}
        col_parts[PAGE_ORDER[0]] = ((0, HALF), (HALF, N))
        for name, copy, tiles in (("first", nc.scalar.copy, PAGE_ORDER[:1]), ("rest", nc.vector.tensor_copy, PAGE_ORDER[1:])):
            n_t = len(tiles)
            z_g = sbuf("z_g_" + name, [P, n_t * PACK * P], BF16)
            z_w = sbuf("z_w_" + name, [P, n_t * P], U32)
            z_s = sbuf("z_s_" + name, [P, n_t * P], U8)
            copy(z_g[:].rearrange("p (t m j) -> p m t j", t=n_t, j=PACK), z_dealt[:, :, tiles[0] : tiles[0] + n_t, :])
            nc.vector.quantize_mx(z_w[:].bitcast(FP8X4), z_s[:], z_g[:])
            for i, t in enumerate(tiles):
                for c0, c1 in col_parts[t]:
                    c_ps[t, c0] = psum.tile([P, c1 - c0], F32, name="c_ps%d_%d" % (t, c0), tag="bank%d" % (t + c0 // HALF))
                    product(c_ps[t, c0][:], z_w, z_s, i, z2_w[:, c0:c1], z2_s[:, c0:c1])

        warm_silu = sbuf("warm_silu", [P, 1], F32)
        nc.scalar.activation(warm_silu[:], z_rows[:, PACK - 1, 0:1], ACT.Silu)

        old_buffers = dict(zip(PAGE_ORDER, ("pa%d" % (PACK - 2), "z_g_rest", "z_w_rest", "z_s_rest")))
        old_h = {}

        def fetch_old(t):
            old_h[t] = sbuf("old_h%d" % t, [P, N], F32, reuse=old_buffers[t])
            nc.scalar.activation(old_h[t][:], page[t][:].indirect(n3_l[:]), ACT.Copy, scale=-0.5)

        fetch_old(PAGE_ORDER[0])
        th = [sbuf("th%d" % t, [P, N], F32) for t in range(PACK)]
        su = [sbuf("su%d" % t, [P, N], F32) for t in range(PACK)]
        kept = [sbuf("kept%d" % t, [P, N], F32) for t in range(PACK)]
        y_g = sbuf("y_g", [P, U, PACK], BF16)

        def keep_part(t):
            for c0, c1 in col_parts[t]:
                nc.scalar.activation(th[t][:, c0:c1], c_ps[t, c0][:], ACT.Tanh, scale=CV_SCALE / 2)
            if t not in old_h:
                fetch_old(t)
            for c0, c1 in col_parts[t]:
                nc.vector.scalar_tensor_tensor(kept[t][:, c0:c1], th[t][:, c0:c1], -1.0, old_h[t][:, c0:c1], ALU.add, ALU.mult)

        def write_part(t):
            for c0, c1 in col_parts[t]:
                nc.scalar.activation(su[t][:, c0:c1], c_ps[t, c0][:], ACT.Silu, scale=CV_SCALE)
                slots = page[t][:].indirect(n3_l[:, c0 // PER_COL : c1 // PER_COL])
                nc.vector.tensor_tensor(slots, su[t][:, c0:c1], kept[t][:, c0:c1], ALU.add)
            nc.sync.dma_start(out_rows[:, t, :], page[t][:])

        def round_slot(copy, t, cols):
            copy(y_g[:, cols, t], page[t][:, cols])

        first, second, third, last = PAGE_ORDER
        keep_part(first)
        write_part(first)
        keep_part(second)
        for t, t_next in ((second, third), (third, last)):
            keep_part(t_next)
            write_part(t)
        round_slot(nc.scalar.copy, first, slice(0, U))
        write_part(last)
        round_slot(nc.scalar.copy, second, slice(0, U))

        y_w = sbuf("y_w", [P, U], U32)
        y_s = sbuf("y_s", [P, U], U8)
        y_flat = y_g[:].rearrange("p c j -> p (c j)")
        words_out = out_1[0].rearrange("p c r -> p (c r)").bitcast(I32)
        for c0, c1 in Y_CHUNKS:
            cols = slice(c0, c1)
            round_slot(nc.scalar.copy, third, cols)
            round_slot(nc.scalar.copy if c1 == U else nc.vector.tensor_copy, last, cols)
            nc.vector.quantize_mx(y_w[:, cols].bitcast(FP8X4), y_s[:, cols], y_flat[:, PACK * c0 : PACK * c1])
            nc.sync.dma_start(words_out[:, cols], y_w[:, cols].bitcast(I32))
        for q in range(QUADS):
            queue = nc.scalar if q % 2 else nc.sync
            queue.dma_start(out_2[0, 4 * q : 4 * q + 4, :].bitcast(I32), y_s[32 * q : 32 * q + 4, :].bitcast(I32))
